import numpy as np
import ml_dtypes


def mxq(x, axis, fmt="e4m3"):
    dtype, down = {"e4m3": (ml_dtypes.float8_e4m3fn, 7), "e5m2": (ml_dtypes.float8_e5m2, 14)}[fmt]
    v = np.moveaxis(np.asarray(x, np.float32).astype(ml_dtypes.bfloat16).astype(np.float64), axis, -1)
    blocks = v.reshape(v.shape[:-1] + (-1, 32))
    amax = np.abs(blocks).max(-1, keepdims=True)
    byte = np.maximum(np.where(amax > 0, np.frexp(amax)[1] - 1 + 127, 0) - down, 1)
    scale = np.exp2(byte - 127.0)
    codes = (blocks / scale).astype(np.float32).astype(dtype).astype(np.float64)
    return np.moveaxis((codes * scale).reshape(v.shape), -1, axis)


WIDE = False


def mx_kscale(k):
    if not WIDE:
        return np.ones(k)
    levels = np.array([10, -10, 5, -5, 0])
    if k % 512:
        return np.exp2(np.random.permutation(np.resize(levels, k // 32))).repeat(32)
    a = np.empty((k // 512, 16))
    for p in range(k // 512):
        a[p, :8] = np.random.permutation(np.resize(levels, 8))
        for g in range(8):
            far = levels[np.abs(levels - a[p, g]) >= 10]
            a[p, g + 8] = far[np.random.randint(len(far))]
    return np.exp2(a.ravel()).repeat(32)


def f64(x):
    return np.asarray(x).astype(np.float64)


def striped(idx):
    return np.tile(np.asarray(idx).reshape(-1, 16).T, (8, 1)).astype(np.uint16)


def unstriped(offs):
    return offs[:16].T.reshape(-1).astype(np.int64)


E2M1 = np.array([0.0, 0.5, 1.0, 1.5, 2.0, 3.0, 4.0, 6.0, -0.0, -0.5, -1.0, -1.5, -2.0, -3.0, -4.0, -6.0])


def pack_weight(w, fmt):
    k, n = w.shape
    w = f64(np.asarray(w, np.float32).astype(ml_dtypes.bfloat16)).reshape(k // 32, 32, n)
    amax = np.abs(w).max(1)
    if fmt == "e4m3":
        byte = np.frexp(amax)[1] - 1 + 127 - 7
    else:
        mant, ex = np.frexp(amax / 6.0)
        byte = np.where(mant > 0.5, ex, ex - 1) + 127
    byte = np.clip(np.where(amax > 0, byte, 1), 1, 254)
    scaled = (w * np.exp2(127.0 - byte)[:, None, :]).reshape(k, n).astype(np.float32)
    by_word = np.ascontiguousarray(scaled.reshape(k // 512, 128, 4, n).transpose(0, 1, 3, 2))
    if fmt == "e4m3":
        words = by_word.astype(ml_dtypes.float8_e4m3fn).view(np.uint8)
    else:
        c = by_word.astype(ml_dtypes.float4_e2m1fn).view(np.uint8) & 0xF
        words = (c[..., 0::2] | (c[..., 1::2] << 4)).reshape(k // 512, 128, 2 * n)
    return np.ascontiguousarray(words), np.ascontiguousarray(byte.astype(np.uint8).reshape(k // 512, 16, n))


def unpack_weight(words, scales, fmt):
    g, _, n = scales.shape
    words = np.ascontiguousarray(words).reshape(g, 128, n, -1)
    if fmt == "e4m3":
        vals = words.view(ml_dtypes.float8_e4m3fn).astype(np.float64)
    else:
        nib = np.empty((g, 128, n, 4), np.uint8)
        nib[..., 0::2] = words & 0xF
        nib[..., 1::2] = words >> 4
        vals = E2M1[nib]
    vals = vals * np.repeat(np.exp2(scales.astype(np.float64) - 127.0), 8, axis=1)[..., None]
    return vals.transpose(0, 1, 3, 2).reshape(g * 512, n)


def silu(v):
    return v / (1.0 + np.exp(-v))


B, N, T, D, NQ = 1, 512, 4096, 512, 256


def setup_inputs():
    n = np.random.standard_normal
    idx = np.random.permutation(T)[:B * N]
    s = mx_kscale(D)[:, None]
    kp = pack_weight(n((D, T)) / s, "e4m3")
    return {
        "qT": (n((B, D, NQ)) * s * (1.00 / np.sqrt(D))).astype(np.float32),
        "k_words": kp[0],
        "k_scales": kp[1],
        "ns": np.tile(np.random.uniform(0.2, 2.0, 4096), (128, 1)).astype(np.float32),
        "offs": striped(idx),
    }


def reference(qT, k_words, k_scales, ns, offs):
    idx = unstriped(offs)
    pick = lambda x, which: x[:, which].reshape(x.shape[0], B, -1).transpose(1, 0, 2)
    k = unpack_weight(k_words, k_scales, "e4m3")
    kg = pick(k, idx)
    qq = mxq(f64(qT), 1, "e4m3")
    a = qq.transpose(0, 2, 1) @ kg
    y = silu(a) * pick(f64(ns), idx)[:, :1, :]
    return y

@@ -1,0 +1,109 @@
+from contextlib import ExitStack
+
+import concourse.mybir as mybir
+from concourse.masks import make_identity
+
+D, NQ, T, N = 512, 256, 4096, 512
+FLOPS = 2 * NQ * D * N
+BYTES = D * NQ * 4 + D * T + (D // 32) * T + T * 4 + 128 * (N // 16) * 2 + NQ * N * 4
+
+F32 = mybir.dt.float32
+BF16 = mybir.dt.bfloat16
+I32 = mybir.dt.int32
+U32 = mybir.dt.uint32
+U16 = mybir.dt.uint16
+U8 = mybir.dt.uint8
+FP8X4 = mybir.dt.float8_e4m3fn_x4
+SILU = mybir.ActivationFunctionType.Silu
+MULT = mybir.AluOpType.mult
+
+P = 128
+PACK = 4
+CHUNK = 256
+NS_ROW = P - 1
+
+
+def tile_attend_neu_silu_topk_kernel(tc, qT, k_words, k_scales, ns, offs, out):
+    nc = tc.nc
+    with ExitStack() as ctx:
+        held = ctx.enter_context(tc.tile_pool(name="held", bufs=1))
+        psum = ctx.enter_context(tc.psum_pool(name="psum", bufs=1))
+
+        offsets = held.tile([P, N // 16], U16, name="offsets")
+        word_table = held.tile([P, T], I32, name="word_table")
+        scale_table = held.tile([P, T], U8, name="scale_table")
+        ns_table = held.tile([P, T], F32, name="ns_table")
+        q_raw = [held.tile([P, PACK, P], F32, name=f"q_raw{m}") for m in range(NQ // P)]
+        q_rows = qT[0].rearrange("(p t) q -> p t q", t=PACK)
+
+        nc.vector.memset(scale_table[:].bitcast(I32), 0)
+        nc.vector.memset(ns_table[0:NS_ROW, :], 0.0)
+
+        nc.sync.dma_start(offsets[:], offs)
+        nc.sync.dma_start(ns_table[NS_ROW:P, :], ns[0:1, :])
+        nc.sync.dma_start(q_raw[0][:], q_rows[:, :, 0:P])
+        nc.sync.dma_start(word_table[:], k_words[0].rearrange("p n t -> p (n t)").bitcast(I32))
+        nc.sync.dma_start(q_raw[1][:], q_rows[:, :, P : 2 * P])
+        for quad in range(4):
+            nc.scalar.dma_start(
+                scale_table[32 * quad : 32 * quad + 4, :].bitcast(I32),
+                k_scales[0, 4 * quad : 4 * quad + 4, :].bitcast(I32),
+            )
+
+        identity = held.tile([P, P], F32, name="identity")
+        make_identity(nc, identity[:])
+
+        k_planes = held.tile([P, N], U8, name="k_planes", align_bytes=64)
+        nc.vector.tensor_copy(k_planes[:], scale_table[:].indirect(offsets[:]))
+        ns_listed = held.tile([P, N], F32, name="ns_listed")
+        nc.vector.tensor_copy(ns_listed[:], ns_table[:].indirect(offsets[:]))
+
+        q_codes, q_planes = [], []
+
+        def quantise_queries(m):
+            woven = held.tile([P, P, PACK], BF16, name=f"woven{m}", align_bytes=64)
+            nc.scalar.copy(woven[:], q_raw[m][:].rearrange("p t q -> p q t"))
+            codes = held.tile([P, P], U32, name=f"q_codes{m}", align_bytes=64)
+            plane = held.tile([P, P], U8, name=f"q_plane{m}", align_bytes=64)
+            nc.vector.quantize_mx(
+                out=codes[:].bitcast(FP8X4), scales=plane[:], in_=woven[:].rearrange("p q t -> p (q t)")
+            )
+            q_codes.append(codes)
+            q_planes.append(plane)
+
+        quantise_queries(0)
+
+        turned = psum.tile([P, N // P, P], F32, name="turned")
+        for j in range(N // P):
+            nc.tensor.transpose(turned[:, j, :], ns_listed[:, j * P : (j + 1) * P], identity[:])
+        ns_columns = held.tile([P, N // P], F32, name="ns_columns")
+        nc.scalar.copy(ns_columns[:], turned[:, :, NS_ROW])
+        ns_spread = psum.tile([P, N], F32, name="ns_spread")
+        for j in range(N // P):
+            nc.tensor.transpose(
+                ns_spread[:, j * P : (j + 1) * P], ns_columns[:, j : j + 1].to_broadcast([P, P]), identity[:]
+            )
+
+        k_codes = held.tile([P, N], U32, name="k_codes", align_bytes=64)
+        nc.vector.tensor_copy(k_codes[:], word_table[:].bitcast(U32).indirect(offsets[:]))
+
+        quantise_queries(1)
+
+        for m in range(NQ // P):
+            for c in range(N // CHUNK):
+                cols = slice(c * CHUNK, (c + 1) * CHUNK)
+                sums = psum.tile([P, CHUNK], F32, name=f"sums{m}_{c}")
+                nc.tensor.matmul_mx(
+                    out=sums[:],
+                    lhsT=q_codes[m][:].bitcast(FP8X4),
+                    lhsT_scale=q_planes[m][:],
+                    rhs=k_codes[:, cols].bitcast(FP8X4),
+                    rhs_scale=k_planes[:, cols],
+                    start=True,
+                    stop=True,
+                )
+                gated = held.tile([P, CHUNK], F32, name=f"gated{m}_{c}")
+                nc.scalar.activation(gated[:], sums[:], SILU)
+                result = held.tile([P, CHUNK], F32, name=f"result{m}_{c}")
+                nc.vector.tensor_tensor(result[:], gated[:], ns_spread[:, cols], MULT)
+                nc.sync.dma_start(out[0, m * P : (m + 1) * P, cols], result[:])

@@ -37,24 +37,31 @@ def tile_attend_neu_silu_topk_kernel(tc, qT, k_words, k_scales, ns, offs, out):
         q_rows = qT[0].rearrange("(p t) q -> p t q", t=PACK)
 
         nc.vector.memset(scale_table[:].bitcast(I32), 0)
-        nc.vector.memset(ns_table[0:NS_ROW, :], 0.0)
+        warm = held.tile([P, 1], F32, name="warm")
+        nc.vector.memset(warm[:], 0.0)
+        nc.vector.memset(ns_table[0:NS_ROW, :].bitcast(I32), 0)
 
         nc.sync.dma_start(offsets[:], offs)
         nc.sync.dma_start(ns_table[NS_ROW:P, :], ns[0:1, :])
         nc.sync.dma_start(q_raw[0][:], q_rows[:, :, 0:P])
         nc.sync.dma_start(word_table[:], k_words[0].rearrange("p n t -> p (n t)").bitcast(I32))
         nc.sync.dma_start(q_raw[1][:], q_rows[:, :, P : 2 * P])
-        for quad in range(4):
-            nc.scalar.dma_start(
-                scale_table[32 * quad : 32 * quad + 4, :].bitcast(I32),
-                k_scales[0, 4 * quad : 4 * quad + 4, :].bitcast(I32),
-            )
+        nc.scalar.dma_start(scale_table[0:P:8, :].bitcast(I32), k_scales[0].bitcast(I32))
+
+        warmed = held.tile([P, 1], F32, name="warmed")
+        nc.scalar.activation(warmed[:], warm[:], SILU)
 
         identity = held.tile([P, P], F32, name="identity")
         make_identity(nc, identity[:])
 
+        scales_listed = held.tile([P, N], U8, name="scales_listed")
+        nc.vector.tensor_copy(scales_listed[:], scale_table[:].indirect(offsets[:]))
         k_planes = held.tile([P, N], U8, name="k_planes", align_bytes=64)
-        nc.vector.tensor_copy(k_planes[:], scale_table[:].indirect(offsets[:]))
+        for quad in range(4):
+            nc.scalar.dma_start(
+                k_planes[32 * quad : 32 * quad + 4, :].bitcast(I32),
+                scales_listed[32 * quad : 32 * quad + 32 : 8, :].bitcast(I32),
+            )
         ns_listed = held.tile([P, N], F32, name="ns_listed")
         nc.vector.tensor_copy(ns_listed[:], ns_table[:].indirect(offsets[:]))
 

@@ -33,8 +33,7 @@ def tile_attend_neu_silu_topk_kernel(tc, qT, k_words, k_scales, ns, offs, out):
         word_table = held.tile([P, T], I32, name="word_table")
         scale_table = held.tile([P, T], U8, name="scale_table")
         ns_table = held.tile([P, T], F32, name="ns_table")
-        q_raw = [held.tile([P, PACK, P], F32, name=f"q_raw{m}") for m in range(NQ // P)]
-        q_rows = qT[0].rearrange("(p t) q -> p t q", t=PACK)
+        q_raw = held.tile([P, PACK, NQ], F32, name="q_raw")
 
         nc.vector.memset(scale_table[:].bitcast(I32), 0)
         warm = held.tile([P, 1], F32, name="warm")
@@ -43,9 +42,10 @@ def tile_attend_neu_silu_topk_kernel(tc, qT, k_words, k_scales, ns, offs, out):
 
         nc.sync.dma_start(offsets[:], offs)
         nc.sync.dma_start(ns_table[NS_ROW:P, :], ns[0:1, :])
-        nc.sync.dma_start(q_raw[0][:], q_rows[:, :, 0:P])
-        nc.sync.dma_start(word_table[:], k_words[0].rearrange("p n t -> p (n t)").bitcast(I32))
-        nc.sync.dma_start(q_raw[1][:], q_rows[:, :, P : 2 * P])
+        nc.sync.dma_start(q_raw[:], qT[0].rearrange("(p t) q -> p t q", t=PACK))
+        nc.sync.dma_start(
+            word_table[:], k_words[0].rearrange("p n t -> p (n t)").bitcast(I32), max_dma_last_dim=4096
+        )
         nc.scalar.dma_start(scale_table[0:P:8, :].bitcast(I32), k_scales[0].bitcast(I32))
 
         warmed = held.tile([P, 1], F32, name="warmed")
@@ -65,20 +65,13 @@ def tile_attend_neu_silu_topk_kernel(tc, qT, k_words, k_scales, ns, offs, out):
         ns_listed = held.tile([P, N], F32, name="ns_listed")
         nc.vector.tensor_copy(ns_listed[:], ns_table[:].indirect(offsets[:]))
 
-        q_codes, q_planes = [], []
-
-        def quantise_queries(m):
-            woven = held.tile([P, P, PACK], BF16, name=f"woven{m}", align_bytes=64)
-            nc.scalar.copy(woven[:], q_raw[m][:].rearrange("p t q -> p q t"))
-            codes = held.tile([P, P], U32, name=f"q_codes{m}", align_bytes=64)
-            plane = held.tile([P, P], U8, name=f"q_plane{m}", align_bytes=64)
-            nc.vector.quantize_mx(
-                out=codes[:].bitcast(FP8X4), scales=plane[:], in_=woven[:].rearrange("p q t -> p (q t)")
-            )
-            q_codes.append(codes)
-            q_planes.append(plane)
-
-        quantise_queries(0)
+        woven = held.tile([P, NQ, PACK], BF16, name="woven", align_bytes=64)
+        nc.scalar.copy(woven[:], q_raw[:].rearrange("p t q -> p q t"))
+        q_codes = held.tile([P, NQ], U32, name="q_codes", align_bytes=64)
+        q_planes = held.tile([P, NQ], U8, name="q_planes", align_bytes=64)
+        nc.vector.quantize_mx(
+            out=q_codes[:].bitcast(FP8X4), scales=q_planes[:], in_=woven[:].rearrange("p q t -> p (q t)")
+        )
 
         turned = psum.tile([P, N // P, P], F32, name="turned")
         for j in range(N // P):
@@ -94,16 +87,14 @@ def tile_attend_neu_silu_topk_kernel(tc, qT, k_words, k_scales, ns, offs, out):
         k_codes = held.tile([P, N], U32, name="k_codes", align_bytes=64)
         nc.vector.tensor_copy(k_codes[:], word_table[:].bitcast(U32).indirect(offsets[:]))
 
-        quantise_queries(1)
-
         for m in range(NQ // P):
             for c in range(N // CHUNK):
                 cols = slice(c * CHUNK, (c + 1) * CHUNK)
                 sums = psum.tile([P, CHUNK], F32, name=f"sums{m}_{c}")
                 nc.tensor.matmul_mx(
                     out=sums[:],
-                    lhsT=q_codes[m][:].bitcast(FP8X4),
-                    lhsT_scale=q_planes[m][:],
+                    lhsT=q_codes[:, m * P : (m + 1) * P].bitcast(FP8X4),
+                    lhsT_scale=q_planes[:, m * P : (m + 1) * P],
                     rhs=k_codes[:, cols].bitcast(FP8X4),
                     rhs_scale=k_planes[:, cols],
                     start=True,

@@ -33,26 +33,24 @@ def tile_attend_neu_silu_topk_kernel(tc, qT, k_words, k_scales, ns, offs, out):
         word_table = held.tile([P, T], I32, name="word_table")
         scale_table = held.tile([P, T], U8, name="scale_table")
         ns_table = held.tile([P, T], F32, name="ns_table")
-        q_raw = held.tile([P, PACK, NQ], F32, name="q_raw")
+        q_raw = held.tile([P, PACK, NQ], F32, name="q_raw", tag="scalar_input")
 
-        nc.vector.memset(scale_table[:].bitcast(I32), 0)
         warm = held.tile([P, 1], F32, name="warm")
         nc.vector.memset(warm[:], 0.0)
-        nc.vector.memset(ns_table[0:NS_ROW, :].bitcast(I32), 0)
+        nc.vector.memset(scale_table[0:48, :].bitcast(I32), 0)
+        nc.vector.memset(scale_table[64:P, :].bitcast(I32), 0)
+        nc.vector.memset(ns_table[0:NS_ROW, 0 : T // 2].bitcast(I32), 0)
 
         nc.sync.dma_start(offsets[:], offs)
+        nc.sync.dma_start(scale_table[48:64, :].bitcast(I32), k_scales[0].bitcast(I32))
         nc.sync.dma_start(ns_table[NS_ROW:P, :], ns[0:1, :])
         nc.sync.dma_start(q_raw[:], qT[0].rearrange("(p t) q -> p t q", t=PACK))
-        nc.sync.dma_start(
-            word_table[:], k_words[0].rearrange("p n t -> p (n t)").bitcast(I32), max_dma_last_dim=4096
-        )
-        nc.scalar.dma_start(scale_table[0:P:8, :].bitcast(I32), k_scales[0].bitcast(I32))
-
-        warmed = held.tile([P, 1], F32, name="warmed")
-        nc.scalar.activation(warmed[:], warm[:], SILU)
+        nc.sync.dma_start(word_table[:], k_words[0].rearrange("p n t -> p (n t)").bitcast(I32))
 
         identity = held.tile([P, P], F32, name="identity")
         make_identity(nc, identity[:])
+        warmed = held.tile([P, 1], F32, name="warmed")
+        nc.scalar.activation(warmed[:], warm[:], SILU)
 
         scales_listed = held.tile([P, N], U8, name="scales_listed")
         nc.vector.tensor_copy(scales_listed[:], scale_table[:].indirect(offsets[:]))
@@ -60,8 +58,9 @@ def tile_attend_neu_silu_topk_kernel(tc, qT, k_words, k_scales, ns, offs, out):
         for quad in range(4):
             nc.scalar.dma_start(
                 k_planes[32 * quad : 32 * quad + 4, :].bitcast(I32),
-                scales_listed[32 * quad : 32 * quad + 32 : 8, :].bitcast(I32),
+                scales_listed[48 + 4 * quad : 52 + 4 * quad, :].bitcast(I32),
             )
+        nc.vector.memset(ns_table[0:NS_ROW, T // 2 : T].bitcast(I32), 0)
         ns_listed = held.tile([P, N], F32, name="ns_listed")
         nc.vector.tensor_copy(ns_listed[:], ns_table[:].indirect(offsets[:]))
 
@@ -76,7 +75,7 @@ def tile_attend_neu_silu_topk_kernel(tc, qT, k_words, k_scales, ns, offs, out):
         turned = psum.tile([P, N // P, P], F32, name="turned")
         for j in range(N // P):
             nc.tensor.transpose(turned[:, j, :], ns_listed[:, j * P : (j + 1) * P], identity[:])
-        ns_columns = held.tile([P, N // P], F32, name="ns_columns")
+        ns_columns = held.tile([P, N // P], F32, name="ns_columns", tag="scalar_input")
         nc.scalar.copy(ns_columns[:], turned[:, :, NS_ROW])
         ns_spread = psum.tile([P, N], F32, name="ns_spread")
         for j in range(N // P):

@@ -21,6 +21,7 @@ P = 128
 PACK = 4
 CHUNK = 256
 NS_ROW = P - 1
+ODD_CUT = 513
 
 
 def tile_attend_neu_silu_topk_kernel(tc, qT, k_words, k_scales, ns, offs, out):
@@ -33,19 +34,26 @@ def tile_attend_neu_silu_topk_kernel(tc, qT, k_words, k_scales, ns, offs, out):
         word_table = held.tile([P, T], I32, name="word_table")
         scale_table = held.tile([P, T], U8, name="scale_table")
         ns_table = held.tile([P, T], F32, name="ns_table")
-        q_raw = held.tile([P, PACK, NQ], F32, name="q_raw", tag="scalar_input")
+        q_raw = [
+            held.tile([P, PACK, P], F32, name="q_raw0", tag="scalar_input"),
+            held.tile([P, PACK, P], F32, name="q_raw1"),
+        ]
+        q_rows = qT[0].rearrange("(p t) q -> p t q", t=PACK)
 
         warm = held.tile([P, 1], F32, name="warm")
         nc.vector.memset(warm[:], 0.0)
-        nc.vector.memset(scale_table[0:48, :].bitcast(I32), 0)
-        nc.vector.memset(scale_table[64:P, :].bitcast(I32), 0)
-        nc.vector.memset(ns_table[0:NS_ROW, 0 : T // 2].bitcast(I32), 0)
+        scale_words = scale_table[:].bitcast(I32)
+        for rows in (slice(0, 48), slice(64, P)):
+            for cols in (slice(0, ODD_CUT), slice(ODD_CUT, T // 4)):
+                nc.vector.memset(scale_words[rows, cols], 0)
+        nc.gpsimd.memset(ns_table[0:NS_ROW, :].bitcast(I32), 0)
 
         nc.sync.dma_start(offsets[:], offs)
         nc.sync.dma_start(scale_table[48:64, :].bitcast(I32), k_scales[0].bitcast(I32))
         nc.sync.dma_start(ns_table[NS_ROW:P, :], ns[0:1, :])
-        nc.sync.dma_start(q_raw[:], qT[0].rearrange("(p t) q -> p t q", t=PACK))
+        nc.sync.dma_start(q_raw[0][:], q_rows[:, :, 0:P])
         nc.sync.dma_start(word_table[:], k_words[0].rearrange("p n t -> p (n t)").bitcast(I32))
+        nc.sync.dma_start(q_raw[1][:], q_rows[:, :, P:NQ])
 
         identity = held.tile([P, P], F32, name="identity")
         make_identity(nc, identity[:])
@@ -60,19 +68,22 @@ def tile_attend_neu_silu_topk_kernel(tc, qT, k_words, k_scales, ns, offs, out):
                 k_planes[32 * quad : 32 * quad + 4, :].bitcast(I32),
                 scales_listed[48 + 4 * quad : 52 + 4 * quad, :].bitcast(I32),
             )
-        nc.vector.memset(ns_table[0:NS_ROW, T // 2 : T].bitcast(I32), 0)
-        ns_listed = held.tile([P, N], F32, name="ns_listed")
+        ns_listed = held.tile([P, N], F32, name="ns_listed", tag="ns_then_queries", align_bytes=64)
         nc.vector.tensor_copy(ns_listed[:], ns_table[:].indirect(offsets[:]))
 
-        woven = held.tile([P, NQ, PACK], BF16, name="woven", align_bytes=64)
-        nc.scalar.copy(woven[:], q_raw[:].rearrange("p t q -> p q t"))
-        q_codes = held.tile([P, NQ], U32, name="q_codes", align_bytes=64)
-        q_planes = held.tile([P, NQ], U8, name="q_planes", align_bytes=64)
-        nc.vector.quantize_mx(
-            out=q_codes[:].bitcast(FP8X4), scales=q_planes[:], in_=woven[:].rearrange("p q t -> p (q t)")
-        )
+        def quantise_queries(m, tag):
+            woven = held.tile([P, P, PACK], BF16, name=f"woven{m}", tag=tag, align_bytes=64)
+            nc.scalar.copy(woven[:], q_raw[m][:].rearrange("p t q -> p q t"))
+            codes = held.tile([P, P], U32, name=f"q_codes{m}", align_bytes=64)
+            planes = held.tile([P, P], U8, name=f"q_planes{m}", align_bytes=64)
+            nc.vector.quantize_mx(
+                out=codes[:].bitcast(FP8X4), scales=planes[:], in_=woven[:].rearrange("p q t -> p (q t)")
+            )
+            return codes, planes
 
-        turned = psum.tile([P, N // P, P], F32, name="turned")
+        queries = [quantise_queries(0, "woven0")]
+
+        turned = psum.tile([P, N // P, P], F32, name="turned", tag="sums0_0")
         for j in range(N // P):
             nc.tensor.transpose(turned[:, j, :], ns_listed[:, j * P : (j + 1) * P], identity[:])
         ns_columns = held.tile([P, N // P], F32, name="ns_columns", tag="scalar_input")
@@ -85,15 +96,16 @@ def tile_attend_neu_silu_topk_kernel(tc, qT, k_words, k_scales, ns, offs, out):
 
         k_codes = held.tile([P, N], U32, name="k_codes", align_bytes=64)
         nc.vector.tensor_copy(k_codes[:], word_table[:].bitcast(U32).indirect(offsets[:]))
+        queries.append(quantise_queries(1, "ns_then_queries"))
 
-        for m in range(NQ // P):
+        for m, (q_codes, q_planes) in enumerate(queries):
             for c in range(N // CHUNK):
                 cols = slice(c * CHUNK, (c + 1) * CHUNK)
                 sums = psum.tile([P, CHUNK], F32, name=f"sums{m}_{c}")
                 nc.tensor.matmul_mx(
                     out=sums[:],
-                    lhsT=q_codes[:, m * P : (m + 1) * P].bitcast(FP8X4),
-                    lhsT_scale=q_planes[:, m * P : (m + 1) * P],
+                    lhsT=q_codes[:].bitcast(FP8X4),
+                    lhsT_scale=q_planes[:],
                     rhs=k_codes[:, cols].bitcast(FP8X4),
                     rhs_scale=k_planes[:, cols],
                     start=True,

@@ -19,7 +19,7 @@ MULT = mybir.AluOpType.mult
 
 P = 128
 PACK = 4
-CHUNK = 256
+CHUNKS = ((128, 128, 256), (256, 128, 128))
 NS_ROW = P - 1
 ODD_CUT = 513
 
@@ -35,7 +35,7 @@ def tile_attend_neu_silu_topk_kernel(tc, qT, k_words, k_scales, ns, offs, out):
         scale_table = held.tile([P, T], U8, name="scale_table")
         ns_table = held.tile([P, T], F32, name="ns_table")
         q_raw = [
-            held.tile([P, PACK, P], F32, name="q_raw0", tag="scalar_input"),
+            held.tile([P, PACK, P], F32, name="q_raw0"),
             held.tile([P, PACK, P], F32, name="q_raw1"),
         ]
         q_rows = qT[0].rearrange("(p t) q -> p t q", t=PACK)
@@ -48,11 +48,11 @@ def tile_attend_neu_silu_topk_kernel(tc, qT, k_words, k_scales, ns, offs, out):
                 nc.vector.memset(scale_words[rows, cols], 0)
         nc.gpsimd.memset(ns_table[0:NS_ROW, :].bitcast(I32), 0)
 
-        nc.sync.dma_start(offsets[:], offs)
-        nc.sync.dma_start(scale_table[48:64, :].bitcast(I32), k_scales[0].bitcast(I32))
         nc.sync.dma_start(ns_table[NS_ROW:P, :], ns[0:1, :])
-        nc.sync.dma_start(q_raw[0][:], q_rows[:, :, 0:P])
+        nc.sync.dma_start(scale_table[48:64, :].bitcast(I32), k_scales[0].bitcast(I32))
+        nc.sync.dma_start(offsets[:], offs)
         nc.sync.dma_start(word_table[:], k_words[0].rearrange("p n t -> p (n t)").bitcast(I32))
+        nc.sync.dma_start(q_raw[0][:], q_rows[:, :, 0:P])
         nc.sync.dma_start(q_raw[1][:], q_rows[:, :, P:NQ])
 
         identity = held.tile([P, P], F32, name="identity")
@@ -81,12 +81,10 @@ def tile_attend_neu_silu_topk_kernel(tc, qT, k_words, k_scales, ns, offs, out):
             )
             return codes, planes
 
-        queries = [quantise_queries(0, "woven0")]
-
         turned = psum.tile([P, N // P, P], F32, name="turned", tag="sums0_0")
         for j in range(N // P):
             nc.tensor.transpose(turned[:, j, :], ns_listed[:, j * P : (j + 1) * P], identity[:])
-        ns_columns = held.tile([P, N // P], F32, name="ns_columns", tag="scalar_input")
+        ns_columns = held.tile([P, N // P], F32, name="ns_columns")
         nc.scalar.copy(ns_columns[:], turned[:, :, NS_ROW])
         ns_spread = psum.tile([P, N], F32, name="ns_spread")
         for j in range(N // P):
@@ -96,12 +94,13 @@ def tile_attend_neu_silu_topk_kernel(tc, qT, k_words, k_scales, ns, offs, out):
 
         k_codes = held.tile([P, N], U32, name="k_codes", align_bytes=64)
         nc.vector.tensor_copy(k_codes[:], word_table[:].bitcast(U32).indirect(offsets[:]))
-        queries.append(quantise_queries(1, "ns_then_queries"))
+        queries = [quantise_queries(0, "ns_then_queries"), quantise_queries(1, "woven1")]
 
         for m, (q_codes, q_planes) in enumerate(queries):
-            for c in range(N // CHUNK):
-                cols = slice(c * CHUNK, (c + 1) * CHUNK)
-                sums = psum.tile([P, CHUNK], F32, name=f"sums{m}_{c}")
+            for c, width in enumerate(CHUNKS[m]):
+                first = sum(CHUNKS[m][:c])
+                cols = slice(first, first + width)
+                sums = psum.tile([P, width], F32, name=f"sums{m}_{c}")
                 nc.tensor.matmul_mx(
                     out=sums[:],
                     lhsT=q_codes[:].bitcast(FP8X4),
@@ -111,8 +110,8 @@ def tile_attend_neu_silu_topk_kernel(tc, qT, k_words, k_scales, ns, offs, out):
                     start=True,
                     stop=True,
                 )
-                gated = held.tile([P, CHUNK], F32, name=f"gated{m}_{c}")
+                gated = held.tile([P, width], F32, name=f"gated{m}_{c}")
                 nc.scalar.activation(gated[:], sums[:], SILU)
-                result = held.tile([P, CHUNK], F32, name=f"result{m}_{c}")
+                result = held.tile([P, width], F32, name=f"result{m}_{c}")
                 nc.vector.tensor_tensor(result[:], gated[:], ns_spread[:, cols], MULT)
                 nc.sync.dma_start(out[0, m * P : (m + 1) * P, cols], result[:])

@@ -21,7 +21,6 @@ P = 128
 PACK = 4
 CHUNKS = ((128, 128, 256), (256, 128, 128))
 NS_ROW = P - 1
-ODD_CUT = 513
 
 
 def tile_attend_neu_silu_topk_kernel(tc, qT, k_words, k_scales, ns, offs, out):
@@ -42,11 +41,9 @@ def tile_attend_neu_silu_topk_kernel(tc, qT, k_words, k_scales, ns, offs, out):
 
         warm = held.tile([P, 1], F32, name="warm")
         nc.vector.memset(warm[:], 0.0)
-        scale_words = scale_table[:].bitcast(I32)
-        for rows in (slice(0, 48), slice(64, P)):
-            for cols in (slice(0, ODD_CUT), slice(ODD_CUT, T // 4)):
-                nc.vector.memset(scale_words[rows, cols], 0)
-        nc.gpsimd.memset(ns_table[0:NS_ROW, :].bitcast(I32), 0)
+        nc.vector.memset(scale_table[0:48, :].bitcast(I32), 0)
+        nc.vector.memset(scale_table[64:P, :].bitcast(I32), 0)
+        nc.vector.memset(ns_table[0:NS_ROW, :].bitcast(I32), 0)
 
         nc.sync.dma_start(ns_table[NS_ROW:P, :], ns[0:1, :])
         nc.sync.dma_start(scale_table[48:64, :].bitcast(I32), k_scales[0].bitcast(I32))

@@ -21,6 +21,7 @@ P = 128
 PACK = 4
 CHUNKS = ((128, 128, 256), (256, 128, 128))
 NS_ROW = P - 1
+GPSIMD_COLUMNS = 3328
 
 
 def tile_attend_neu_silu_topk_kernel(tc, qT, k_words, k_scales, ns, offs, out):
@@ -30,26 +31,30 @@ def tile_attend_neu_silu_topk_kernel(tc, qT, k_words, k_scales, ns, offs, out):
         psum = ctx.enter_context(tc.psum_pool(name="psum", bufs=1))
 
         offsets = held.tile([P, N // 16], U16, name="offsets")
-        word_table = held.tile([P, T], I32, name="word_table")
+        word_table = held.tile([P, T], I32, name="word_table", tag="words_then_codes", align_bytes=64)
         scale_table = held.tile([P, T], U8, name="scale_table")
         ns_table = held.tile([P, T], F32, name="ns_table")
-        q_raw = [
-            held.tile([P, PACK, P], F32, name="q_raw0"),
-            held.tile([P, PACK, P], F32, name="q_raw1"),
-        ]
+        q_raw = [held.tile([P, PACK, P], F32, name=f"q_raw{m}") for m in range(NQ // P)]
         q_rows = qT[0].rearrange("(p t) q -> p t q", t=PACK)
 
         warm = held.tile([P, 1], F32, name="warm")
         nc.vector.memset(warm[:], 0.0)
-        nc.vector.memset(scale_table[0:48, :].bitcast(I32), 0)
-        nc.vector.memset(scale_table[64:P, :].bitcast(I32), 0)
-        nc.vector.memset(ns_table[0:NS_ROW, :].bitcast(I32), 0)
+        nc.gpsimd.memset(ns_table[0:NS_ROW, 0:GPSIMD_COLUMNS], 0.0)
+
+        def zero_in_odd_widths(words):
+            half = words.shape[1] // 2
+            nc.vector.memset(words[:, 0 : half + 1], 0)
+            nc.vector.memset(words[:, half + 1 :], 0)
+
+        zero_in_odd_widths(ns_table[0:NS_ROW, GPSIMD_COLUMNS:T].bitcast(I32))
+        zero_in_odd_widths(scale_table[0:48, :].bitcast(I32))
+        zero_in_odd_widths(scale_table[64:P, :].bitcast(I32))
 
         nc.sync.dma_start(ns_table[NS_ROW:P, :], ns[0:1, :])
-        nc.sync.dma_start(scale_table[48:64, :].bitcast(I32), k_scales[0].bitcast(I32))
         nc.sync.dma_start(offsets[:], offs)
-        nc.sync.dma_start(word_table[:], k_words[0].rearrange("p n t -> p (n t)").bitcast(I32))
+        nc.sync.dma_start(scale_table[48:64, :].bitcast(I32), k_scales[0].bitcast(I32))
         nc.sync.dma_start(q_raw[0][:], q_rows[:, :, 0:P])
+        nc.sync.dma_start(word_table[:], k_words[0].rearrange("p n t -> p (n t)").bitcast(I32))
         nc.sync.dma_start(q_raw[1][:], q_rows[:, :, P:NQ])
 
         identity = held.tile([P, P], F32, name="identity")
@@ -57,26 +62,28 @@ def tile_attend_neu_silu_topk_kernel(tc, qT, k_words, k_scales, ns, offs, out):
         warmed = held.tile([P, 1], F32, name="warmed")
         nc.scalar.activation(warmed[:], warm[:], SILU)
 
+        ns_listed = held.tile([P, N], F32, name="ns_listed", tag="ns_then_queries", align_bytes=64)
+        nc.vector.tensor_copy(ns_listed[:], ns_table[:].indirect(offsets[:]))
         scales_listed = held.tile([P, N], U8, name="scales_listed")
         nc.vector.tensor_copy(scales_listed[:], scale_table[:].indirect(offsets[:]))
         k_planes = held.tile([P, N], U8, name="k_planes", align_bytes=64)
         for quad in range(4):
-            nc.scalar.dma_start(
+            nc.sync.dma_start(
                 k_planes[32 * quad : 32 * quad + 4, :].bitcast(I32),
                 scales_listed[48 + 4 * quad : 52 + 4 * quad, :].bitcast(I32),
             )
-        ns_listed = held.tile([P, N], F32, name="ns_listed", tag="ns_then_queries", align_bytes=64)
-        nc.vector.tensor_copy(ns_listed[:], ns_table[:].indirect(offsets[:]))
 
-        def quantise_queries(m, tag):
-            woven = held.tile([P, P, PACK], BF16, name=f"woven{m}", tag=tag, align_bytes=64)
+        def quantise_queries(m, woven_tag, codes_tag):
+            woven = held.tile([P, P, PACK], BF16, name=f"woven{m}", tag=woven_tag, align_bytes=64)
             nc.scalar.copy(woven[:], q_raw[m][:].rearrange("p t q -> p q t"))
-            codes = held.tile([P, P], U32, name=f"q_codes{m}", align_bytes=64)
+            codes = held.tile([P, P], U32, name=f"q_codes{m}", tag=codes_tag, align_bytes=64)
             planes = held.tile([P, P], U8, name=f"q_planes{m}", align_bytes=64)
             nc.vector.quantize_mx(
                 out=codes[:].bitcast(FP8X4), scales=planes[:], in_=woven[:].rearrange("p q t -> p (q t)")
             )
             return codes, planes
+
+        queries = [quantise_queries(0, "woven0", "q_codes0")]
 
         turned = psum.tile([P, N // P, P], F32, name="turned", tag="sums0_0")
         for j in range(N // P):
@@ -91,7 +98,7 @@ def tile_attend_neu_silu_topk_kernel(tc, qT, k_words, k_scales, ns, offs, out):
 
         k_codes = held.tile([P, N], U32, name="k_codes", align_bytes=64)
         nc.vector.tensor_copy(k_codes[:], word_table[:].bitcast(U32).indirect(offsets[:]))
-        queries = [quantise_queries(0, "ns_then_queries"), quantise_queries(1, "woven1")]
+        queries.append(quantise_queries(1, "ns_then_queries", "words_then_codes"))
 
         for m, (q_codes, q_planes) in enumerate(queries):
             for c, width in enumerate(CHUNKS[m]):

@@ -46,13 +46,13 @@ def tile_attend_neu_silu_topk_kernel(tc, qT, k_words, k_scales, ns, offs, out):
             nc.vector.memset(words[:, 0 : half + 1], 0)
             nc.vector.memset(words[:, half + 1 :], 0)
 
-        zero_in_odd_widths(ns_table[0:NS_ROW, GPSIMD_COLUMNS:T].bitcast(I32))
         zero_in_odd_widths(scale_table[0:48, :].bitcast(I32))
         zero_in_odd_widths(scale_table[64:P, :].bitcast(I32))
+        zero_in_odd_widths(ns_table[0:NS_ROW, GPSIMD_COLUMNS:T].bitcast(I32))
 
-        nc.sync.dma_start(ns_table[NS_ROW:P, :], ns[0:1, :])
-        nc.sync.dma_start(offsets[:], offs)
         nc.sync.dma_start(scale_table[48:64, :].bitcast(I32), k_scales[0].bitcast(I32))
+        nc.sync.dma_start(offsets[:], offs)
+        nc.sync.dma_start(ns_table[NS_ROW:P, :], ns[0:1, :])
         nc.sync.dma_start(q_raw[0][:], q_rows[:, :, 0:P])
         nc.sync.dma_start(word_table[:], k_words[0].rearrange("p n t -> p (n t)").bitcast(I32))
         nc.sync.dma_start(q_raw[1][:], q_rows[:, :, P:NQ])
@@ -62,8 +62,6 @@ def tile_attend_neu_silu_topk_kernel(tc, qT, k_words, k_scales, ns, offs, out):
         warmed = held.tile([P, 1], F32, name="warmed")
         nc.scalar.activation(warmed[:], warm[:], SILU)
 
-        ns_listed = held.tile([P, N], F32, name="ns_listed", tag="ns_then_queries", align_bytes=64)
-        nc.vector.tensor_copy(ns_listed[:], ns_table[:].indirect(offsets[:]))
         scales_listed = held.tile([P, N], U8, name="scales_listed")
         nc.vector.tensor_copy(scales_listed[:], scale_table[:].indirect(offsets[:]))
         k_planes = held.tile([P, N], U8, name="k_planes", align_bytes=64)
@@ -72,6 +70,8 @@ def tile_attend_neu_silu_topk_kernel(tc, qT, k_words, k_scales, ns, offs, out):
                 k_planes[32 * quad : 32 * quad + 4, :].bitcast(I32),
                 scales_listed[48 + 4 * quad : 52 + 4 * quad, :].bitcast(I32),
             )
+        ns_listed = held.tile([P, N], F32, name="ns_listed", tag="ns_then_queries", align_bytes=64)
+        nc.vector.tensor_copy(ns_listed[:], ns_table[:].indirect(offsets[:]))
 
         def quantise_queries(m, woven_tag, codes_tag):
             woven = held.tile([P, P, PACK], BF16, name=f"woven{m}", tag=woven_tag, align_bytes=64)
@@ -85,16 +85,18 @@ def tile_attend_neu_silu_topk_kernel(tc, qT, k_words, k_scales, ns, offs, out):
 
         queries = [quantise_queries(0, "woven0", "q_codes0")]
 
-        turned = psum.tile([P, N // P, P], F32, name="turned", tag="sums0_0")
-        for j in range(N // P):
-            nc.tensor.transpose(turned[:, j, :], ns_listed[:, j * P : (j + 1) * P], identity[:])
-        ns_columns = held.tile([P, N // P], F32, name="ns_columns")
-        nc.scalar.copy(ns_columns[:], turned[:, :, NS_ROW])
+        ns_columns = []
+        for half in range(2):
+            turned = psum.tile([P, 2, P], F32, name=f"turned{half}", tag=f"sums0_{half}")
+            for j in range(2):
+                first = (2 * half + j) * P
+                nc.tensor.transpose(turned[:, j, :], ns_listed[:, first : first + P], identity[:])
+            columns = held.tile([P, 2], F32, name=f"ns_columns{half}")
+            nc.scalar.copy(columns[:], turned[:, :, NS_ROW])
+            ns_columns.extend(columns[:, j : j + 1] for j in range(2))
         ns_spread = psum.tile([P, N], F32, name="ns_spread")
-        for j in range(N // P):
-            nc.tensor.transpose(
-                ns_spread[:, j * P : (j + 1) * P], ns_columns[:, j : j + 1].to_broadcast([P, P]), identity[:]
-            )
+        for j, column in enumerate(ns_columns):
+            nc.tensor.transpose(ns_spread[:, j * P : (j + 1) * P], column.to_broadcast([P, P]), identity[:])
 
         k_codes = held.tile([P, N], U32, name="k_codes", align_bytes=64)
         nc.vector.tensor_copy(k_codes[:], word_table[:].bitcast(U32).indirect(offsets[:]))

@@ -19,9 +19,13 @@ MULT = mybir.AluOpType.mult
 
 P = 128
 PACK = 4
-CHUNKS = ((128, 128, 256), (256, 128, 128))
+QUADRANT = 32
+ROWS_PER_QUADRANT = 4
+SCALE_ROWS = slice(48, 64)
 NS_ROW = P - 1
 GPSIMD_COLUMNS = 3328
+CHUNKS = ((128, 128, 256), (128, 256, 128))
+TURNS_PER_BANK = 2
 
 
 def tile_attend_neu_silu_topk_kernel(tc, qT, k_words, k_scales, ns, offs, out):
@@ -33,7 +37,7 @@ def tile_attend_neu_silu_topk_kernel(tc, qT, k_words, k_scales, ns, offs, out):
         offsets = held.tile([P, N // 16], U16, name="offsets")
         word_table = held.tile([P, T], I32, name="word_table", tag="words_then_codes", align_bytes=64)
         scale_table = held.tile([P, T], U8, name="scale_table")
-        ns_table = held.tile([P, T], F32, name="ns_table")
+        ns_table = held.tile([P, T], F32, name="ns_table", tag="ns_then_codes", align_bytes=64)
         q_raw = [held.tile([P, PACK, P], F32, name=f"q_raw{m}") for m in range(NQ // P)]
         q_rows = qT[0].rearrange("(p t) q -> p t q", t=PACK)
 
@@ -46,14 +50,14 @@ def tile_attend_neu_silu_topk_kernel(tc, qT, k_words, k_scales, ns, offs, out):
             nc.vector.memset(words[:, 0 : half + 1], 0)
             nc.vector.memset(words[:, half + 1 :], 0)
 
-        zero_in_odd_widths(scale_table[0:48, :].bitcast(I32))
-        zero_in_odd_widths(scale_table[64:P, :].bitcast(I32))
+        zero_in_odd_widths(scale_table[0 : SCALE_ROWS.start, :].bitcast(I32))
+        zero_in_odd_widths(scale_table[SCALE_ROWS.stop : P, :].bitcast(I32))
         zero_in_odd_widths(ns_table[0:NS_ROW, GPSIMD_COLUMNS:T].bitcast(I32))
 
-        nc.sync.dma_start(scale_table[48:64, :].bitcast(I32), k_scales[0].bitcast(I32))
+        nc.sync.dma_start(q_raw[0][:], q_rows[:, :, 0:P])
+        nc.sync.dma_start(scale_table[SCALE_ROWS, :].bitcast(I32), k_scales[0].bitcast(I32))
         nc.sync.dma_start(offsets[:], offs)
         nc.sync.dma_start(ns_table[NS_ROW:P, :], ns[0:1, :])
-        nc.sync.dma_start(q_raw[0][:], q_rows[:, :, 0:P])
         nc.sync.dma_start(word_table[:], k_words[0].rearrange("p n t -> p (n t)").bitcast(I32))
         nc.sync.dma_start(q_raw[1][:], q_rows[:, :, P:NQ])
 
@@ -65,10 +69,11 @@ def tile_attend_neu_silu_topk_kernel(tc, qT, k_words, k_scales, ns, offs, out):
         scales_listed = held.tile([P, N], U8, name="scales_listed")
         nc.vector.tensor_copy(scales_listed[:], scale_table[:].indirect(offsets[:]))
         k_planes = held.tile([P, N], U8, name="k_planes", align_bytes=64)
-        for quad in range(4):
+        for quad in range(P // QUADRANT):
+            source = SCALE_ROWS.start + ROWS_PER_QUADRANT * quad
             nc.sync.dma_start(
-                k_planes[32 * quad : 32 * quad + 4, :].bitcast(I32),
-                scales_listed[48 + 4 * quad : 52 + 4 * quad, :].bitcast(I32),
+                k_planes[QUADRANT * quad : QUADRANT * quad + ROWS_PER_QUADRANT, :].bitcast(I32),
+                scales_listed[source : source + ROWS_PER_QUADRANT, :].bitcast(I32),
             )
         ns_listed = held.tile([P, N], F32, name="ns_listed", tag="ns_then_queries", align_bytes=64)
         nc.vector.tensor_copy(ns_listed[:], ns_table[:].indirect(offsets[:]))
@@ -83,17 +88,17 @@ def tile_attend_neu_silu_topk_kernel(tc, qT, k_words, k_scales, ns, offs, out):
             )
             return codes, planes
 
-        queries = [quantise_queries(0, "woven0", "q_codes0")]
+        queries = [quantise_queries(0, "woven0", "ns_then_codes")]
 
         ns_columns = []
-        for half in range(2):
-            turned = psum.tile([P, 2, P], F32, name=f"turned{half}", tag=f"sums0_{half}")
-            for j in range(2):
-                first = (2 * half + j) * P
-                nc.tensor.transpose(turned[:, j, :], ns_listed[:, first : first + P], identity[:])
-            columns = held.tile([P, 2], F32, name=f"ns_columns{half}")
+        for bank in range(N // P // TURNS_PER_BANK):
+            turned = psum.tile([P, TURNS_PER_BANK, P], F32, name=f"turned{bank}", tag=f"sums0_{bank}")
+            for j in range(TURNS_PER_BANK):
+                block = (TURNS_PER_BANK * bank + j) * P
+                nc.tensor.transpose(turned[:, j, :], ns_listed[:, block : block + P], identity[:])
+            columns = held.tile([P, TURNS_PER_BANK], F32, name=f"ns_columns{bank}")
             nc.scalar.copy(columns[:], turned[:, :, NS_ROW])
-            ns_columns.extend(columns[:, j : j + 1] for j in range(2))
+            ns_columns.extend(columns[:, j : j + 1] for j in range(TURNS_PER_BANK))
         ns_spread = psum.tile([P, N], F32, name="ns_spread")
         for j, column in enumerate(ns_columns):
             nc.tensor.transpose(ns_spread[:, j * P : (j + 1) * P], column.to_broadcast([P, P]), identity[:])

@@ -24,7 +24,9 @@ ROWS_PER_QUADRANT = 4
 SCALE_ROWS = slice(48, 64)
 NS_ROW = P - 1
 GPSIMD_COLUMNS = 3328
-CHUNKS = ((128, 128, 256), (128, 256, 128))
+CHUNK = 128
+STORES = ((128, 128, 256), (256, 128, 128))
+SUM_BANKS = 7
 TURNS_PER_BANK = 2
 
 
@@ -92,7 +94,7 @@ def tile_attend_neu_silu_topk_kernel(tc, qT, k_words, k_scales, ns, offs, out):
 
         ns_columns = []
         for bank in range(N // P // TURNS_PER_BANK):
-            turned = psum.tile([P, TURNS_PER_BANK, P], F32, name=f"turned{bank}", tag=f"sums0_{bank}")
+            turned = psum.tile([P, TURNS_PER_BANK, P], F32, name=f"turned{bank}", tag=f"bank{bank}")
             for j in range(TURNS_PER_BANK):
                 block = (TURNS_PER_BANK * bank + j) * P
                 nc.tensor.transpose(turned[:, j, :], ns_listed[:, block : block + P], identity[:])
@@ -108,10 +110,13 @@ def tile_attend_neu_silu_topk_kernel(tc, qT, k_words, k_scales, ns, offs, out):
         queries.append(quantise_queries(1, "ns_then_queries", "words_then_codes"))
 
         for m, (q_codes, q_planes) in enumerate(queries):
-            for c, width in enumerate(CHUNKS[m]):
-                first = sum(CHUNKS[m][:c])
-                cols = slice(first, first + width)
-                sums = psum.tile([P, width], F32, name=f"sums{m}_{c}")
+            gated = held.tile([P, N], F32, name=f"gated{m}")
+            result = held.tile([P, N], F32, name=f"result{m}")
+            ends = {sum(STORES[m][: s + 1]): width for s, width in enumerate(STORES[m])}
+            for c in range(N // CHUNK):
+                cols = slice(c * CHUNK, (c + 1) * CHUNK)
+                bank = (m * (N // CHUNK) + c) % SUM_BANKS
+                sums = psum.tile([P, CHUNK], F32, name=f"sums{m}_{c}", tag=f"bank{bank}")
                 nc.tensor.matmul_mx(
                     out=sums[:],
                     lhsT=q_codes[:].bitcast(FP8X4),
@@ -121,8 +126,8 @@ def tile_attend_neu_silu_topk_kernel(tc, qT, k_words, k_scales, ns, offs, out):
                     start=True,
                     stop=True,
                 )
-                gated = held.tile([P, width], F32, name=f"gated{m}_{c}")
-                nc.scalar.activation(gated[:], sums[:], SILU)
-                result = held.tile([P, width], F32, name=f"result{m}_{c}")
-                nc.vector.tensor_tensor(result[:], gated[:], ns_spread[:, cols], MULT)
-                nc.sync.dma_start(out[0, m * P : (m + 1) * P, cols], result[:])
+                nc.scalar.activation(gated[:, cols], sums[:], SILU)
+                nc.vector.tensor_tensor(result[:, cols], gated[:, cols], ns_spread[:, cols], MULT)
+                if cols.stop in ends:
+                    stored = slice(cols.stop - ends[cols.stop], cols.stop)
+                    nc.sync.dma_start(out[0, m * P : (m + 1) * P, stored], result[:, stored])

@@ -23,11 +23,11 @@ QUADRANT = 32
 ROWS_PER_QUADRANT = 4
 SCALE_ROWS = slice(48, 64)
 NS_ROW = P - 1
-GPSIMD_COLUMNS = 3328
+GPSIMD_COLUMNS = 2752
 CHUNK = 128
 STORES = ((128, 128, 256), (256, 128, 128))
 SUM_BANKS = 7
-TURNS_PER_BANK = 2
+TURNS_PER_BANK = 1
 
 
 def tile_attend_neu_silu_topk_kernel(tc, qT, k_words, k_scales, ns, offs, out):
@@ -39,12 +39,16 @@ def tile_attend_neu_silu_topk_kernel(tc, qT, k_words, k_scales, ns, offs, out):
         offsets = held.tile([P, N // 16], U16, name="offsets")
         word_table = held.tile([P, T], I32, name="word_table", tag="words_then_codes", align_bytes=64)
         scale_table = held.tile([P, T], U8, name="scale_table")
-        ns_table = held.tile([P, T], F32, name="ns_table", tag="ns_then_codes", align_bytes=64)
-        q_raw = [held.tile([P, PACK, P], F32, name=f"q_raw{m}") for m in range(NQ // P)]
+        ns_table = held.tile([P, T], F32, name="ns_table")
+        q_raw = [
+            held.tile([P, PACK, P], F32, name=f"q_raw{m}", tag=tag, align_bytes=64)
+            for m, tag in enumerate(("q_raw0", "queries_then_gated"))
+        ]
         q_rows = qT[0].rearrange("(p t) q -> p t q", t=PACK)
 
         warm = held.tile([P, 1], F32, name="warm")
         nc.vector.memset(warm[:], 0.0)
+        nc.gpsimd.memset(scale_table[SCALE_ROWS.stop : P, :].bitcast(I32), 0)
         nc.gpsimd.memset(ns_table[0:NS_ROW, 0:GPSIMD_COLUMNS], 0.0)
 
         def zero_in_odd_widths(words):
@@ -53,13 +57,12 @@ def tile_attend_neu_silu_topk_kernel(tc, qT, k_words, k_scales, ns, offs, out):
             nc.vector.memset(words[:, half + 1 :], 0)
 
         zero_in_odd_widths(scale_table[0 : SCALE_ROWS.start, :].bitcast(I32))
-        zero_in_odd_widths(scale_table[SCALE_ROWS.stop : P, :].bitcast(I32))
         zero_in_odd_widths(ns_table[0:NS_ROW, GPSIMD_COLUMNS:T].bitcast(I32))
 
-        nc.sync.dma_start(q_raw[0][:], q_rows[:, :, 0:P])
         nc.sync.dma_start(scale_table[SCALE_ROWS, :].bitcast(I32), k_scales[0].bitcast(I32))
+        nc.scalar.dma_start(ns_table[NS_ROW:P, :], ns[0:1, :])
+        nc.sync.dma_start(q_raw[0][:], q_rows[:, :, 0:P])
         nc.sync.dma_start(offsets[:], offs)
-        nc.sync.dma_start(ns_table[NS_ROW:P, :], ns[0:1, :])
         nc.sync.dma_start(word_table[:], k_words[0].rearrange("p n t -> p (n t)").bitcast(I32))
         nc.sync.dma_start(q_raw[1][:], q_rows[:, :, P:NQ])
 
@@ -90,7 +93,7 @@ def tile_attend_neu_silu_topk_kernel(tc, qT, k_words, k_scales, ns, offs, out):
             )
             return codes, planes
 
-        queries = [quantise_queries(0, "woven0", "ns_then_codes")]
+        queries = [quantise_queries(0, "woven0", "q_codes0")]
 
         ns_columns = []
         for bank in range(N // P // TURNS_PER_BANK):
@@ -110,8 +113,8 @@ def tile_attend_neu_silu_topk_kernel(tc, qT, k_words, k_scales, ns, offs, out):
         queries.append(quantise_queries(1, "ns_then_queries", "words_then_codes"))
 
         for m, (q_codes, q_planes) in enumerate(queries):
-            gated = held.tile([P, N], F32, name=f"gated{m}")
-            result = held.tile([P, N], F32, name=f"result{m}")
+            gated = held.tile([P, N], F32, name=f"gated{m}", tag=("queries_then_gated", "gated1")[m], align_bytes=64)
+            result = held.tile([P, N], F32, name=f"result{m}", tag=("ns_then_queries", "result1")[m], align_bytes=64)
             ends = {sum(STORES[m][: s + 1]): width for s, width in enumerate(STORES[m])}
             for c in range(N // CHUNK):
                 cols = slice(c * CHUNK, (c + 1) * CHUNK)

@@ -109,7 +109,9 @@ def tile_attend_neu_silu_topk_kernel(tc, qT, k_words, k_scales, ns, offs, out):
             nc.tensor.transpose(ns_spread[:, j * P : (j + 1) * P], column.to_broadcast([P, P]), identity[:])
 
         k_codes = held.tile([P, N], U32, name="k_codes", align_bytes=64)
-        nc.vector.tensor_copy(k_codes[:], word_table[:].bitcast(U32).indirect(offsets[:]))
+        for half in (slice(0, N // 2), slice(N // 2, N)):
+            part = offsets[:, half.start // 16 : half.stop // 16]
+            nc.vector.tensor_copy(k_codes[:, half], word_table[:].bitcast(U32).indirect(part))
         queries.append(quantise_queries(1, "ns_then_queries", "words_then_codes"))
 
         for m, (q_codes, q_planes) in enumerate(queries):

@@ -83,9 +83,20 @@ def tile_attend_neu_silu_topk_kernel(tc, qT, k_words, k_scales, ns, offs, out):
         ns_listed = held.tile([P, N], F32, name="ns_listed", tag="ns_then_queries", align_bytes=64)
         nc.vector.tensor_copy(ns_listed[:], ns_table[:].indirect(offsets[:]))
 
-        def quantise_queries(m, woven_tag, codes_tag):
+        def by_lines(ap, order):
+            return ap.rearrange(order, i=PACK)
+
+        def quantise_queries(m, woven_tag, codes_tag, vector_share=0):
             woven = held.tile([P, P, PACK], BF16, name=f"woven{m}", tag=woven_tag, align_bytes=64)
-            nc.scalar.copy(woven[:], q_raw[m][:].rearrange("p t q -> p q t"))
+            cut = P - vector_share
+            nc.scalar.copy(
+                by_lines(woven[:, 0:cut, :], "p (c i) t -> p c t i"), by_lines(q_raw[m][:, :, 0:cut], "p t (c i) -> p c t i")
+            )
+            if vector_share:
+                nc.vector.tensor_copy(
+                    by_lines(woven[:, cut:P, :], "p (c i) t -> p c t i"),
+                    by_lines(q_raw[m][:, :, cut:P], "p t (c i) -> p c t i"),
+                )
             codes = held.tile([P, P], U32, name=f"q_codes{m}", tag=codes_tag, align_bytes=64)
             planes = held.tile([P, P], U8, name=f"q_planes{m}", align_bytes=64)
             nc.vector.quantize_mx(
@@ -112,11 +123,11 @@ def tile_attend_neu_silu_topk_kernel(tc, qT, k_words, k_scales, ns, offs, out):
         for half in (slice(0, N // 2), slice(N // 2, N)):
             part = offsets[:, half.start // 16 : half.stop // 16]
             nc.vector.tensor_copy(k_codes[:, half], word_table[:].bitcast(U32).indirect(part))
-        queries.append(quantise_queries(1, "ns_then_queries", "words_then_codes"))
+        queries.append(quantise_queries(1, "ns_then_queries", "words_then_codes", vector_share=32))
 
         for m, (q_codes, q_planes) in enumerate(queries):
-            gated = held.tile([P, N], F32, name=f"gated{m}", tag=("queries_then_gated", "gated1")[m], align_bytes=64)
-            result = held.tile([P, N], F32, name=f"result{m}", tag=("ns_then_queries", "result1")[m], align_bytes=64)
+            gated = held.tile([P, N], F32, name=f"gated{m}", align_bytes=64)
+            result = held.tile([P, N], F32, name=f"result{m}", align_bytes=64)
             ends = {sum(STORES[m][: s + 1]): width for s, width in enumerate(STORES[m])}
             for c in range(N // CHUNK):
                 cols = slice(c * CHUNK, (c + 1) * CHUNK)

@@ -37,7 +37,7 @@ def tile_attend_neu_silu_topk_kernel(tc, qT, k_words, k_scales, ns, offs, out):
         psum = ctx.enter_context(tc.psum_pool(name="psum", bufs=1))
 
         offsets = held.tile([P, N // 16], U16, name="offsets")
-        word_table = held.tile([P, T], I32, name="word_table", tag="words_then_codes", align_bytes=64)
+        word_table = held.tile([P, T], I32, name="word_table")
         scale_table = held.tile([P, T], U8, name="scale_table")
         ns_table = held.tile([P, T], F32, name="ns_table")
         q_raw = [
@@ -86,17 +86,11 @@ def tile_attend_neu_silu_topk_kernel(tc, qT, k_words, k_scales, ns, offs, out):
         def by_lines(ap, order):
             return ap.rearrange(order, i=PACK)
 
-        def quantise_queries(m, woven_tag, codes_tag, vector_share=0):
+        def quantise_queries(m, woven_tag, codes_tag):
             woven = held.tile([P, P, PACK], BF16, name=f"woven{m}", tag=woven_tag, align_bytes=64)
-            cut = P - vector_share
             nc.scalar.copy(
-                by_lines(woven[:, 0:cut, :], "p (c i) t -> p c t i"), by_lines(q_raw[m][:, :, 0:cut], "p t (c i) -> p c t i")
+                by_lines(woven[:], "p (c i) t -> p c t i"), by_lines(q_raw[m][:], "p t (c i) -> p c t i")
             )
-            if vector_share:
-                nc.vector.tensor_copy(
-                    by_lines(woven[:, cut:P, :], "p (c i) t -> p c t i"),
-                    by_lines(q_raw[m][:, :, cut:P], "p t (c i) -> p c t i"),
-                )
             codes = held.tile([P, P], U32, name=f"q_codes{m}", tag=codes_tag, align_bytes=64)
             planes = held.tile([P, P], U8, name=f"q_planes{m}", align_bytes=64)
             nc.vector.quantize_mx(
@@ -123,7 +117,7 @@ def tile_attend_neu_silu_topk_kernel(tc, qT, k_words, k_scales, ns, offs, out):
         for half in (slice(0, N // 2), slice(N // 2, N)):
             part = offsets[:, half.start // 16 : half.stop // 16]
             nc.vector.tensor_copy(k_codes[:, half], word_table[:].bitcast(U32).indirect(part))
-        queries.append(quantise_queries(1, "ns_then_queries", "words_then_codes", vector_share=32))
+        queries.append(quantise_queries(1, "ns_then_queries", "q_codes1"))
 
         for m, (q_codes, q_planes) in enumerate(queries):
             gated = held.tile([P, N], F32, name=f"gated{m}", align_bytes=64)

@@ -37,11 +37,11 @@ def tile_attend_neu_silu_topk_kernel(tc, qT, k_words, k_scales, ns, offs, out):
         psum = ctx.enter_context(tc.psum_pool(name="psum", bufs=1))
 
         offsets = held.tile([P, N // 16], U16, name="offsets")
-        word_table = held.tile([P, T], I32, name="word_table")
-        scale_table = held.tile([P, T], U8, name="scale_table")
-        ns_table = held.tile([P, T], F32, name="ns_table")
+        word_table = held.tile([P, T], I32, name="word_table", align_bytes=256)
+        scale_table = held.tile([P, T], U8, name="scale_table", align_bytes=256)
+        ns_table = held.tile([P, T], F32, name="ns_table", align_bytes=256)
         q_raw = [
-            held.tile([P, PACK, P], F32, name=f"q_raw{m}", tag=tag, align_bytes=64)
+            held.tile([P, PACK, P], F32, name=f"q_raw{m}", tag=tag, align_bytes=256)
             for m, tag in enumerate(("q_raw0", "queries_then_gated"))
         ]
         q_rows = qT[0].rearrange("(p t) q -> p t q", t=PACK)
@@ -71,9 +71,9 @@ def tile_attend_neu_silu_topk_kernel(tc, qT, k_words, k_scales, ns, offs, out):
         warmed = held.tile([P, 1], F32, name="warmed")
         nc.scalar.activation(warmed[:], warm[:], SILU)
 
-        scales_listed = held.tile([P, N], U8, name="scales_listed")
+        scales_listed = held.tile([P, N], U8, name="scales_listed", align_bytes=256)
         nc.vector.tensor_copy(scales_listed[:], scale_table[:].indirect(offsets[:]))
-        k_planes = held.tile([P, N], U8, name="k_planes", align_bytes=64)
+        k_planes = held.tile([P, N], U8, name="k_planes", align_bytes=256)
         for quad in range(P // QUADRANT):
             source = SCALE_ROWS.start + ROWS_PER_QUADRANT * quad
             nc.sync.dma_start(
@@ -121,7 +121,7 @@ def tile_attend_neu_silu_topk_kernel(tc, qT, k_words, k_scales, ns, offs, out):
 
         for m, (q_codes, q_planes) in enumerate(queries):
             gated = held.tile([P, N], F32, name=f"gated{m}", align_bytes=64)
-            result = held.tile([P, N], F32, name=f"result{m}", align_bytes=64)
+            result = held.tile([P, N], F32, name=f"result{m}", align_bytes=256)
             ends = {sum(STORES[m][: s + 1]): width for s, width in enumerate(STORES[m])}
             for c in range(N // CHUNK):
                 cols = slice(c * CHUNK, (c + 1) * CHUNK)

@@ -25,9 +25,11 @@ SCALE_ROWS = slice(48, 64)
 NS_ROW = P - 1
 GPSIMD_COLUMNS = 2752
 CHUNK = 128
-STORES = ((128, 128, 256), (256, 128, 128))
-SUM_BANKS = 7
-TURNS_PER_BANK = 1
+PER_TILE = N // CHUNK
+GROUPS = ((0,), (1,), (2,), (3,), (4, 5), (6,), (7,))
+GPSIMD_CHUNKS = ()
+STORES = ((256, 256), (256, 128, 128))
+SLABS = (1, 2)
 
 
 def tile_attend_neu_silu_topk_kernel(tc, qT, k_words, k_scales, ns, offs, out):
@@ -41,10 +43,16 @@ def tile_attend_neu_silu_topk_kernel(tc, qT, k_words, k_scales, ns, offs, out):
         scale_table = held.tile([P, T], U8, name="scale_table", align_bytes=256)
         ns_table = held.tile([P, T], F32, name="ns_table", align_bytes=256)
         q_raw = [
-            held.tile([P, PACK, P], F32, name=f"q_raw{m}", tag=tag, align_bytes=256)
-            for m, tag in enumerate(("q_raw0", "queries_then_gated"))
+            [held.tile([P, PACK, P // slabs], F32, name=f"q_raw{m}_{s}", align_bytes=256) for s in range(slabs)]
+            for m, slabs in enumerate(SLABS)
         ]
         q_rows = qT[0].rearrange("(p t) q -> p t q", t=PACK)
+
+        def load_queries(m):
+            width = P // SLABS[m]
+            for s, slab in enumerate(q_raw[m]):
+                first = m * P + s * width
+                nc.sync.dma_start(slab[:], q_rows[:, :, first : first + width])
 
         warm = held.tile([P, 1], F32, name="warm")
         nc.vector.memset(warm[:], 0.0)
@@ -61,10 +69,10 @@ def tile_attend_neu_silu_topk_kernel(tc, qT, k_words, k_scales, ns, offs, out):
 
         nc.sync.dma_start(scale_table[SCALE_ROWS, :].bitcast(I32), k_scales[0].bitcast(I32))
         nc.scalar.dma_start(ns_table[NS_ROW:P, :], ns[0:1, :])
-        nc.sync.dma_start(q_raw[0][:], q_rows[:, :, 0:P])
+        load_queries(0)
         nc.sync.dma_start(offsets[:], offs)
         nc.sync.dma_start(word_table[:], k_words[0].rearrange("p n t -> p (n t)").bitcast(I32))
-        nc.sync.dma_start(q_raw[1][:], q_rows[:, :, P:NQ])
+        load_queries(1)
 
         identity = held.tile([P, P], F32, name="identity")
         make_identity(nc, identity[:])
@@ -86,49 +94,55 @@ def tile_attend_neu_silu_topk_kernel(tc, qT, k_words, k_scales, ns, offs, out):
         def by_lines(ap, order):
             return ap.rearrange(order, i=PACK)
 
-        def quantise_queries(m, woven_tag, codes_tag):
+        def quantise_queries(m, woven_tag):
             woven = held.tile([P, P, PACK], BF16, name=f"woven{m}", tag=woven_tag, align_bytes=64)
-            nc.scalar.copy(
-                by_lines(woven[:], "p (c i) t -> p c t i"), by_lines(q_raw[m][:], "p t (c i) -> p c t i")
-            )
-            codes = held.tile([P, P], U32, name=f"q_codes{m}", tag=codes_tag, align_bytes=64)
+            width = P // SLABS[m]
+            for s, slab in enumerate(q_raw[m]):
+                nc.scalar.copy(
+                    by_lines(woven[:, s * width : (s + 1) * width, :], "p (c i) t -> p c t i"),
+                    by_lines(slab[:], "p t (c i) -> p c t i"),
+                )
+            codes = held.tile([P, P], U32, name=f"q_codes{m}", align_bytes=64)
             planes = held.tile([P, P], U8, name=f"q_planes{m}", align_bytes=64)
             nc.vector.quantize_mx(
                 out=codes[:].bitcast(FP8X4), scales=planes[:], in_=woven[:].rearrange("p q t -> p (q t)")
             )
             return codes, planes
 
-        queries = [quantise_queries(0, "woven0", "q_codes0")]
+        queries = [quantise_queries(0, "woven0")]
 
         ns_columns = []
-        for bank in range(N // P // TURNS_PER_BANK):
-            turned = psum.tile([P, TURNS_PER_BANK, P], F32, name=f"turned{bank}", tag=f"bank{bank}")
-            for j in range(TURNS_PER_BANK):
-                block = (TURNS_PER_BANK * bank + j) * P
-                nc.tensor.transpose(turned[:, j, :], ns_listed[:, block : block + P], identity[:])
-            columns = held.tile([P, TURNS_PER_BANK], F32, name=f"ns_columns{bank}")
-            nc.scalar.copy(columns[:], turned[:, :, NS_ROW])
-            ns_columns.extend(columns[:, j : j + 1] for j in range(TURNS_PER_BANK))
+        for block in range(PER_TILE):
+            turned = psum.tile([P, P], F32, name=f"turned{block}", tag=f"bank{block}")
+            nc.tensor.transpose(turned[:], ns_listed[:, block * P : (block + 1) * P], identity[:])
+            column = held.tile([P, 1], F32, name=f"ns_column{block}")
+            nc.scalar.copy(column[:], turned[:, NS_ROW:P])
+            ns_columns.append(column)
         ns_spread = psum.tile([P, N], F32, name="ns_spread")
         for j, column in enumerate(ns_columns):
-            nc.tensor.transpose(ns_spread[:, j * P : (j + 1) * P], column.to_broadcast([P, P]), identity[:])
+            nc.tensor.transpose(ns_spread[:, j * P : (j + 1) * P], column[:].to_broadcast([P, P]), identity[:])
+        ns_copies = {}
+        for c in GPSIMD_CHUNKS:
+            j = c % PER_TILE
+            ns_copies[c] = held.tile([P, CHUNK], F32, name=f"ns_copy{c}")
+            nc.scalar.copy(ns_copies[c][:], ns_spread[:, j * CHUNK : (j + 1) * CHUNK])
 
         k_codes = held.tile([P, N], U32, name="k_codes", align_bytes=64)
         for half in (slice(0, N // 2), slice(N // 2, N)):
             part = offsets[:, half.start // 16 : half.stop // 16]
             nc.vector.tensor_copy(k_codes[:, half], word_table[:].bitcast(U32).indirect(part))
-        queries.append(quantise_queries(1, "ns_then_queries", "q_codes1"))
+        queries.append(quantise_queries(1, "ns_then_queries"))
 
-        for m, (q_codes, q_planes) in enumerate(queries):
-            gated = held.tile([P, N], F32, name=f"gated{m}", align_bytes=64)
-            result = held.tile([P, N], F32, name=f"result{m}", align_bytes=256)
-            ends = {sum(STORES[m][: s + 1]): width for s, width in enumerate(STORES[m])}
-            for c in range(N // CHUNK):
-                cols = slice(c * CHUNK, (c + 1) * CHUNK)
-                bank = (m * (N // CHUNK) + c) % SUM_BANKS
-                sums = psum.tile([P, CHUNK], F32, name=f"sums{m}_{c}", tag=f"bank{bank}")
+        gated = held.tile([P, NQ // P * N], F32, name="gated", align_bytes=64)
+        results = [held.tile([P, N], F32, name=f"result{m}", align_bytes=256) for m in range(NQ // P)]
+        ends = [{sum(widths[: s + 1]): w for s, w in enumerate(widths)} for widths in STORES]
+        for g, group in enumerate(GROUPS):
+            sums = psum.tile([P, len(group) * CHUNK], F32, name=f"sums{g}", tag=f"bank{g % 7}")
+            for place, c in enumerate(group):
+                q_codes, q_planes = queries[c // PER_TILE]
+                cols = slice(c % PER_TILE * CHUNK, (c % PER_TILE + 1) * CHUNK)
                 nc.tensor.matmul_mx(
-                    out=sums[:],
+                    out=sums[:, place * CHUNK : (place + 1) * CHUNK],
                     lhsT=q_codes[:].bitcast(FP8X4),
                     lhsT_scale=q_planes[:],
                     rhs=k_codes[:, cols].bitcast(FP8X4),
@@ -136,8 +150,15 @@ def tile_attend_neu_silu_topk_kernel(tc, qT, k_words, k_scales, ns, offs, out):
                     start=True,
                     stop=True,
                 )
-                nc.scalar.activation(gated[:, cols], sums[:], SILU)
-                nc.vector.tensor_tensor(result[:, cols], gated[:, cols], ns_spread[:, cols], MULT)
-                if cols.stop in ends:
-                    stored = slice(cols.stop - ends[cols.stop], cols.stop)
-                    nc.sync.dma_start(out[0, m * P : (m + 1) * P, stored], result[:, stored])
+            nc.scalar.activation(gated[:, group[0] * CHUNK : (group[-1] + 1) * CHUNK], sums[:], SILU)
+            for c in group:
+                m = c // PER_TILE
+                cols = slice(c % PER_TILE * CHUNK, (c % PER_TILE + 1) * CHUNK)
+                source = gated[:, c * CHUNK : (c + 1) * CHUNK]
+                if c in GPSIMD_CHUNKS:
+                    nc.gpsimd.tensor_tensor(results[m][:, cols], source, ns_copies[c][:], MULT)
+                else:
+                    nc.vector.tensor_tensor(results[m][:, cols], source, ns_spread[:, cols], MULT)
+                if cols.stop in ends[m]:
+                    stored = slice(cols.stop - ends[m][cols.stop], cols.stop)
+                    nc.sync.dma_start(out[0, m * P : (m + 1) * P, stored], results[m][:, stored])

@@ -16,6 +16,7 @@ U8 = mybir.dt.uint8
 FP8X4 = mybir.dt.float8_e4m3fn_x4
 SILU = mybir.ActivationFunctionType.Silu
 MULT = mybir.AluOpType.mult
+ADD = mybir.AluOpType.add
 
 P = 128
 PACK = 4
@@ -26,10 +27,10 @@ NS_ROW = P - 1
 GPSIMD_COLUMNS = 2752
 CHUNK = 128
 PER_TILE = N // CHUNK
-GROUPS = ((0,), (1,), (2,), (3,), (4, 5), (6,), (7,))
+GROUPS = ((0,), (1,), (2,), (3,), (4,), (5,), (6,), (7,))
 GPSIMD_CHUNKS = ()
-STORES = ((256, 256), (256, 128, 128))
-SLABS = (1, 2)
+STORES = ((128, 128, 256), (256, 128, 128))
+GPSIMD_QUERIES = (0, 48)
 
 
 def tile_attend_neu_silu_topk_kernel(tc, qT, k_words, k_scales, ns, offs, out):
@@ -40,19 +41,15 @@ def tile_attend_neu_silu_topk_kernel(tc, qT, k_words, k_scales, ns, offs, out):
 
         offsets = held.tile([P, N // 16], U16, name="offsets")
         word_table = held.tile([P, T], I32, name="word_table", align_bytes=256)
-        scale_table = held.tile([P, T], U8, name="scale_table", align_bytes=256)
+        scale_table = held.tile([P, T], U8, name="scale_table", tag="scales_then_queries", align_bytes=256)
         ns_table = held.tile([P, T], F32, name="ns_table", align_bytes=256)
-        q_raw = [
-            [held.tile([P, PACK, P // slabs], F32, name=f"q_raw{m}_{s}", align_bytes=256) for s in range(slabs)]
-            for m, slabs in enumerate(SLABS)
-        ]
+        q_raw = []
         q_rows = qT[0].rearrange("(p t) q -> p t q", t=PACK)
 
-        def load_queries(m):
-            width = P // SLABS[m]
-            for s, slab in enumerate(q_raw[m]):
-                first = m * P + s * width
-                nc.sync.dma_start(slab[:], q_rows[:, :, first : first + width])
+        def load_queries(m, tag):
+            raw = held.tile([P, PACK, P], F32, name=f"q_raw{m}", tag=tag, align_bytes=256)
+            nc.sync.dma_start(raw[:], q_rows[:, :, m * P : (m + 1) * P])
+            q_raw.append(raw)
 
         warm = held.tile([P, 1], F32, name="warm")
         nc.vector.memset(warm[:], 0.0)
@@ -69,10 +66,9 @@ def tile_attend_neu_silu_topk_kernel(tc, qT, k_words, k_scales, ns, offs, out):
 
         nc.sync.dma_start(scale_table[SCALE_ROWS, :].bitcast(I32), k_scales[0].bitcast(I32))
         nc.scalar.dma_start(ns_table[NS_ROW:P, :], ns[0:1, :])
-        load_queries(0)
+        load_queries(0, "q_raw0")
         nc.sync.dma_start(offsets[:], offs)
         nc.sync.dma_start(word_table[:], k_words[0].rearrange("p n t -> p (n t)").bitcast(I32))
-        load_queries(1)
 
         identity = held.tile([P, P], F32, name="identity")
         make_identity(nc, identity[:])
@@ -88,6 +84,7 @@ def tile_attend_neu_silu_topk_kernel(tc, qT, k_words, k_scales, ns, offs, out):
                 k_planes[QUADRANT * quad : QUADRANT * quad + ROWS_PER_QUADRANT, :].bitcast(I32),
                 scales_listed[source : source + ROWS_PER_QUADRANT, :].bitcast(I32),
             )
+        load_queries(1, "scales_then_queries")
         ns_listed = held.tile([P, N], F32, name="ns_listed", tag="ns_then_queries", align_bytes=64)
         nc.vector.tensor_copy(ns_listed[:], ns_table[:].indirect(offsets[:]))
 
@@ -96,11 +93,19 @@ def tile_attend_neu_silu_topk_kernel(tc, qT, k_words, k_scales, ns, offs, out):
 
         def quantise_queries(m, woven_tag):
             woven = held.tile([P, P, PACK], BF16, name=f"woven{m}", tag=woven_tag, align_bytes=64)
-            width = P // SLABS[m]
-            for s, slab in enumerate(q_raw[m]):
-                nc.scalar.copy(
-                    by_lines(woven[:, s * width : (s + 1) * width, :], "p (c i) t -> p c t i"),
-                    by_lines(slab[:], "p t (c i) -> p c t i"),
+            split = P - GPSIMD_QUERIES[m]
+            nc.scalar.copy(
+                by_lines(woven[:, 0:split, :], "p (c i) t -> p c t i"),
+                by_lines(q_raw[m][:, :, 0:split], "p t (c i) -> p c t i"),
+            )
+            if split < P:
+                nc.gpsimd.tensor_scalar(
+                    by_lines(woven[:, split:P, :], "p (c i) t -> p c t i"),
+                    by_lines(q_raw[m][:, :, split:P], "p t (c i) -> p c t i"),
+                    1.0,
+                    0.0,
+                    MULT,
+                    ADD,
                 )
             codes = held.tile([P, P], U32, name=f"q_codes{m}", align_bytes=64)
             planes = held.tile([P, P], U8, name=f"q_planes{m}", align_bytes=64)

from contextlib import ExitStack

import concourse.mybir as mybir
from concourse.masks import make_identity

D, NQ, T, N = 512, 256, 4096, 512
FLOPS = 2 * NQ * D * N
BYTES = D * NQ * 4 + D * T + (D // 32) * T + T * 4 + 128 * (N // 16) * 2 + NQ * N * 4

F32 = mybir.dt.float32
BF16 = mybir.dt.bfloat16
I32 = mybir.dt.int32
U32 = mybir.dt.uint32
U16 = mybir.dt.uint16
U8 = mybir.dt.uint8
FP8X4 = mybir.dt.float8_e4m3fn_x4
SILU = mybir.ActivationFunctionType.Silu
MULT = mybir.AluOpType.mult
ADD = mybir.AluOpType.add

P = 128
PACK = 4
QUADRANT = 32
ROWS_PER_QUADRANT = 4
SCALE_ROWS = slice(48, 64)
NS_ROW = P - 1
GPSIMD_COLUMNS = 2752
CHUNK = 128
PER_TILE = N // CHUNK
GROUPS = ((0,), (1,), (2,), (3,), (4,), (5,), (6,), (7,))
GPSIMD_CHUNKS = ()
STORES = ((128, 128, 256), (256, 128, 128))
GPSIMD_QUERIES = (0, 48)


def tile_attend_neu_silu_topk_kernel(tc, qT, k_words, k_scales, ns, offs, out):
    nc = tc.nc
    with ExitStack() as ctx:
        held = ctx.enter_context(tc.tile_pool(name="held", bufs=1))
        psum = ctx.enter_context(tc.psum_pool(name="psum", bufs=1))

        offsets = held.tile([P, N // 16], U16, name="offsets")
        word_table = held.tile([P, T], I32, name="word_table", align_bytes=256)
        scale_table = held.tile([P, T], U8, name="scale_table", tag="scales_then_queries", align_bytes=256)
        ns_table = held.tile([P, T], F32, name="ns_table", align_bytes=256)
        q_raw = []
        q_rows = qT[0].rearrange("(p t) q -> p t q", t=PACK)

        def load_queries(m, tag):
            raw = held.tile([P, PACK, P], F32, name=f"q_raw{m}", tag=tag, align_bytes=256)
            nc.sync.dma_start(raw[:], q_rows[:, :, m * P : (m + 1) * P])
            q_raw.append(raw)

        warm = held.tile([P, 1], F32, name="warm")
        nc.vector.memset(warm[:], 0.0)
        nc.gpsimd.memset(scale_table[SCALE_ROWS.stop : P, :].bitcast(I32), 0)
        nc.gpsimd.memset(ns_table[0:NS_ROW, 0:GPSIMD_COLUMNS], 0.0)

        def zero_in_odd_widths(words):
            half = words.shape[1] // 2
            nc.vector.memset(words[:, 0 : half + 1], 0)
            nc.vector.memset(words[:, half + 1 :], 0)

        zero_in_odd_widths(scale_table[0 : SCALE_ROWS.start, :].bitcast(I32))
        zero_in_odd_widths(ns_table[0:NS_ROW, GPSIMD_COLUMNS:T].bitcast(I32))

        nc.sync.dma_start(scale_table[SCALE_ROWS, :].bitcast(I32), k_scales[0].bitcast(I32))
        nc.scalar.dma_start(ns_table[NS_ROW:P, :], ns[0:1, :])
        load_queries(0, "q_raw0")
        nc.sync.dma_start(offsets[:], offs)
        nc.sync.dma_start(word_table[:], k_words[0].rearrange("p n t -> p (n t)").bitcast(I32))

        identity = held.tile([P, P], F32, name="identity")
        make_identity(nc, identity[:])
        warmed = held.tile([P, 1], F32, name="warmed")
        nc.scalar.activation(warmed[:], warm[:], SILU)

        scales_listed = held.tile([P, N], U8, name="scales_listed", align_bytes=256)
        nc.vector.tensor_copy(scales_listed[:], scale_table[:].indirect(offsets[:]))
        k_planes = held.tile([P, N], U8, name="k_planes", align_bytes=256)
        for quad in range(P // QUADRANT):
            source = SCALE_ROWS.start + ROWS_PER_QUADRANT * quad
            nc.sync.dma_start(
                k_planes[QUADRANT * quad : QUADRANT * quad + ROWS_PER_QUADRANT, :].bitcast(I32),
                scales_listed[source : source + ROWS_PER_QUADRANT, :].bitcast(I32),
            )
        load_queries(1, "scales_then_queries")
        ns_listed = held.tile([P, N], F32, name="ns_listed", tag="ns_then_queries", align_bytes=64)
        nc.vector.tensor_copy(ns_listed[:], ns_table[:].indirect(offsets[:]))

        def by_lines(ap, order):
            return ap.rearrange(order, i=PACK)

        def quantise_queries(m, woven_tag):
            woven = held.tile([P, P, PACK], BF16, name=f"woven{m}", tag=woven_tag, align_bytes=64)
            split = P - GPSIMD_QUERIES[m]
            nc.scalar.copy(
                by_lines(woven[:, 0:split, :], "p (c i) t -> p c t i"),
                by_lines(q_raw[m][:, :, 0:split], "p t (c i) -> p c t i"),
            )
            if split < P:
                nc.gpsimd.tensor_scalar(
                    by_lines(woven[:, split:P, :], "p (c i) t -> p c t i"),
                    by_lines(q_raw[m][:, :, split:P], "p t (c i) -> p c t i"),
                    1.0,
                    0.0,
                    MULT,
                    ADD,
                )
            codes = held.tile([P, P], U32, name=f"q_codes{m}", align_bytes=64)
            planes = held.tile([P, P], U8, name=f"q_planes{m}", align_bytes=64)
            nc.vector.quantize_mx(
                out=codes[:].bitcast(FP8X4), scales=planes[:], in_=woven[:].rearrange("p q t -> p (q t)")
            )
            return codes, planes

        queries = [quantise_queries(0, "woven0")]

        ns_columns = []
        for block in range(PER_TILE):
            turned = psum.tile([P, P], F32, name=f"turned{block}", tag=f"bank{block}")
            nc.tensor.transpose(turned[:], ns_listed[:, block * P : (block + 1) * P], identity[:])
            column = held.tile([P, 1], F32, name=f"ns_column{block}")
            nc.scalar.copy(column[:], turned[:, NS_ROW:P])
            ns_columns.append(column)
        ns_spread = psum.tile([P, N], F32, name="ns_spread")
        for j, column in enumerate(ns_columns):
            nc.tensor.transpose(ns_spread[:, j * P : (j + 1) * P], column[:].to_broadcast([P, P]), identity[:])
        ns_copies = {}
        for c in GPSIMD_CHUNKS:
            j = c % PER_TILE
            ns_copies[c] = held.tile([P, CHUNK], F32, name=f"ns_copy{c}")
            nc.scalar.copy(ns_copies[c][:], ns_spread[:, j * CHUNK : (j + 1) * CHUNK])

        k_codes = held.tile([P, N], U32, name="k_codes", align_bytes=64)
        for half in (slice(0, N // 2), slice(N // 2, N)):
            part = offsets[:, half.start // 16 : half.stop // 16]
            nc.vector.tensor_copy(k_codes[:, half], word_table[:].bitcast(U32).indirect(part))
        queries.append(quantise_queries(1, "ns_then_queries"))

        gated = held.tile([P, NQ // P * N], F32, name="gated", align_bytes=64)
        results = [held.tile([P, N], F32, name=f"result{m}", align_bytes=256) for m in range(NQ // P)]
        ends = [{sum(widths[: s + 1]): w for s, w in enumerate(widths)} for widths in STORES]
        for g, group in enumerate(GROUPS):
            sums = psum.tile([P, len(group) * CHUNK], F32, name=f"sums{g}", tag=f"bank{g % 7}")
            for place, c in enumerate(group):
                q_codes, q_planes = queries[c // PER_TILE]
                cols = slice(c % PER_TILE * CHUNK, (c % PER_TILE + 1) * CHUNK)
                nc.tensor.matmul_mx(
                    out=sums[:, place * CHUNK : (place + 1) * CHUNK],
                    lhsT=q_codes[:].bitcast(FP8X4),
                    lhsT_scale=q_planes[:],
                    rhs=k_codes[:, cols].bitcast(FP8X4),
                    rhs_scale=k_planes[:, cols],
                    start=True,
                    stop=True,
                )
            nc.scalar.activation(gated[:, group[0] * CHUNK : (group[-1] + 1) * CHUNK], sums[:], SILU)
            for c in group:
                m = c // PER_TILE
                cols = slice(c % PER_TILE * CHUNK, (c % PER_TILE + 1) * CHUNK)
                source = gated[:, c * CHUNK : (c + 1) * CHUNK]
                if c in GPSIMD_CHUNKS:
                    nc.gpsimd.tensor_tensor(results[m][:, cols], source, ns_copies[c][:], MULT)
                else:
                    nc.vector.tensor_tensor(results[m][:, cols], source, ns_spread[:, cols], MULT)
                if cols.stop in ends[m]:
                    stored = slice(cols.stop - ends[m][cols.stop], cols.stop)
                    nc.sync.dma_start(out[0, m * P : (m + 1) * P, stored], results[m][:, stored])
